import numpy as np, ml_dtypes
CORES = [24,40,56,80,88,96]
N = 6
import mx_ref
NC, G, MB = 128, 2, 4
C = np.float32(0.029)
BF = ml_dtypes.bfloat16
def cut(t, i, w=512):
    return t[:, w * i:w * i + w]
def tile(rs):
    return np.stack(rs, axis=2).reshape(128, -1).astype(BF)
def layer(w, X):
    out = []
    for i in range(G):
        for t in range(len(X)):
            p = mx_ref.matmul(mx_ref.quantize(cut(w, len(X) * i + t)), X[t])
            z = p if t == 0 else z + p
        out.append(z)
    return out
def act(Z):
    return [np.maximum(s * z, 0) * C for z in Z for s in (1, -1)]
def setup_inputs(rng):
    def f(*shape):
        return mx_ref.flush((rng.standard_normal(shape, dtype=np.float32) * np.exp2(rng.integers(-2, 3, shape[:-1] + (1,)))).astype(BF))
    return {"x": f(N, 128, MB * 4 * NC), "w1": f(N, 128, G * 512), "w2": f(N, 128, 512)}
def setup_inputs_blocks(rng):
    d = setup_inputs(rng)
    for k in ("x", "w1", "w2"): d[k] = mx_ref.spread(d[k], rng, 4)
    return d
def setup_inputs_wide(rng):
    d = setup_inputs(rng)
    for k in ("x", "w1", "w2"): d[k] = mx_ref.flush((d[k].astype(np.float32) * np.exp2(rng.integers(-8, 9, (N, 1, 1))).astype(np.float32)).astype(BF))
    return d
def setup_inputs_zeros(rng):
    d = setup_inputs(rng); v = d["x"].reshape(N, 128, -1, 4).copy()
    v[np.broadcast_to((rng.random((N, 1, v.shape[2], 1)) < 0.33), v.shape)] = 0
    d["x"] = v.reshape(d["x"].shape)
    return d
def reference(x, w1, w2):
    H = [mx_ref.quantize(tile(act(layer(w1[j], [mx_ref.quantize(cut(x[j], m, 4 * NC))])))) for j in range(N) for m in range(MB)]
    y = np.zeros((N, 128, N * MB * NC), np.float32)
    for r in range(N):
        qw = mx_ref.quantize(w2[r])
        for b in range(N * MB):
            y[r][:, NC * b:NC * b + NC] = mx_ref.matmul(qw, H[b])
    return {"y": y}

@@ -1,0 +1,279 @@
+from concourse.bass import DstId, RemoteDMATransfer
+from concourse.mybir import dt, AluOpType, ActivationFunctionType
+
+N, MB, NC = 6, 4, 128
+NB = N * MB
+SIM_CORES = 112
+C = 0.029
+U8 = dt.uint8
+HS, PS, YS = 3, 3, 2
+ITEMS = ("c0", "p0", "c1", "c2", "p1", "c3")
+
+SCRATCH = {
+    "bw": ("sbuf", [128, 512], "bfloat16"),
+    "bv": ("sbuf", [128, 512], "bfloat16"),
+    "bx": ("sbuf", [128, 512], "bfloat16"),
+    "bh": ("sbuf", [128, 512], "bfloat16"),
+    "xc": ("sbuf", [128, NC], "float8_e4m3fn_x4"),
+    "xp": ("sbuf", [128, NC], "uint8"),
+    "wc": ("sbuf", [128, 2 * NC], "float8_e4m3fn_x4"),
+    "wp": ("sbuf", [128, 2 * NC], "uint8"),
+    "vc": ("sbuf", [128, NC], "float8_e4m3fn_x4"),
+    "vp": ("sbuf", [128, NC], "uint8"),
+    "hc": ("sbuf", [128, HS * NC], "float8_e4m3fn_x4"),
+    "hp": ("sbuf", [128, PS * 2 * NC], "uint8"),
+    "ys": ("sbuf", [128, YS * 2 * NC], "float32"),
+    "ps": ("psum", [128, 8 * 512], "float32"),
+}
+SEMAPHORES = ["lw0", "lw1", "lv", "qw0", "qw1", "qv", "out"]
+SEMAPHORES += ["%s%d" % (_s, _m) for _s in ("lx", "qx", "z0", "z1", "sg", "qh") for _m in range(MB)]
+SEMAPHORES += ["%s%d" % (_s, _k) for _s in ("m", "k") for _k in range(NB)]
+SEMAPHORES += ["f%d" % _k for _k in range(MB, NB)]
+SEMAPHORES += ["y%d" % _s for _s in range(YS)]
+for _i in ITEMS:
+    SEMAPHORES.append("s" + _i)
+    for _j in range(N):
+        SEMAPHORES.append("a%s_%d" % (_i, _j))
+        SCRATCH["d%s_%d" % (_i, _j)] = (("dram", [128, NC], "float8_e4m3fn_x4") if _i[0] == "c"
+                                        else ("dram", [128, 2 * NC], "uint8"))
+
+
+def engines(mask):
+    return [i for i in range(mask.bit_length()) if (mask >> i) & 1]
+
+
+def roads(T, topo, j):
+    home = T.cores[j]
+    own = [c for c in range(SIM_CORES) if topo.chip(c) == topo.chip(home) and c not in T.cores
+           and all(topo.may_write(c, q) for q in T.cores if q != c)]
+    near = [c for c in own if topo.die(c) == topo.die(home)]
+    far = [c for c in own if topo.die(c) != topo.die(home)]
+    rest = [(j + o) % N for o in range(1, N)]
+    same = [r for r in rest if topo.same_plane(topo.chip(T.cores[r]), topo.chip(home))]
+    cross = [r for r in rest if r not in same]
+    off = engines(topo.mask(home, T.cores[cross[0]]))
+    on = [e for e in engines(topo.mask(home, own[0])) if e not in off]
+    if len(same) > len(cross):
+        a, b = cross, same
+    else:
+        a, b = cross[0::2] + same, cross[1::2]
+    first = [(home, None, same, off), (far[0], on, cross, off)]
+    split = [(near[1], on[0::2], a, off), (far[1], on[1::2], b, off)]
+    return {"c0": first, "p0": first,
+            "c1": [(near[0], on, same + cross, off)],
+            "c2": [(far[0], on, same + cross, off)],
+            "p1": split, "c3": split}
+
+
+def send(g, T, topo, item, j, src, parts, local):
+    land = T["d%s_%d" % (item, j)][:]
+    if item[0] == "c":
+        src, land = src.bitcast(U8), land.bitcast(U8)
+    trs = []
+    for es, cores, sem in parts:
+        ids = [topo.addr(c) for c in cores]
+        trs.append(RemoteDMATransfer(dst_ids=[DstId(rid=i[0], pnc=i[1]) for i in ids],
+                                     dma_engine_mask=sum(1 << e for e in es), remote_sem=T.sem[sem],
+                                     srcs=[src], dsts=[land for c in cores]))
+    g.remote_dma_fused(trs, local_sem=local)
+    return sum(len(es) for es, cores, sem in parts)
+
+
+def rank_core(g, core, rank, T, topo):
+    S = T.sem
+    V, P, A, D = g.vector, g.tensor, g.scalar, g.sync
+    F = ActivationFunctionType
+
+    def cols(s, n=NC):
+        return slice(n * s, n * s + n)
+
+    def codes(k):
+        return T.hc[:, cols(k % HS)]
+
+    def plane(k):
+        return T.hp[:, cols(2 * (k // 2 % PS) + k % 2)]
+
+    def bank(b):
+        return T.ps[:, 512 * b:512 * b + NC]
+
+    left = {}
+
+    def ship(item, src):
+        parts = []
+        for carrier, es, ranks, eo in roads(T, topo, rank)[item]:
+            if carrier == core:
+                parts.append((eo, [T.cores[r] for r in ranks], "a%s_%d" % (item, rank)))
+            else:
+                parts.append((es, [carrier], "s" + item))
+        left[item] = send(g, T, topo, item, rank, src, parts, S["s" + item])
+    for m in range(MB):
+        g.wait_ge(S["qh%d" % m], 1)
+        if m % 2:
+            ship("p%d" % (m // 2), T.hp[:, cols(m // 2, 2 * NC)])
+        ship("c%d" % m, codes(m))
+
+    pairs = [(rank, p) for p in range(MB // 2)]
+    for p in range(MB // 2):
+        js = [(rank - o) % N for o in range(1, N)]
+        if p == 0:
+            js.sort(key=lambda j: not topo.same_plane(topo.chip(T.cores[j]), topo.chip(core)))
+        pairs += [(j, p) for j in js]
+
+    def load_x(q, m):
+        q.dma_start(T.bx[:], T.x[:, cols(m, 512)]).then_inc(S["lx%d" % m], 16)
+
+    def load_w(i):
+        D.dma_start(T.bw[:], T.w1[:, cols(i, 512)]).then_inc(S["lw%d" % i], 16)
+
+    def arrived(item, j):
+        n = [len(eo) for c, es, ranks, eo in roads(T, topo, j)[item] if rank in ranks][0]
+        D.wait_ge(S["a%s_%d" % (item, j)], n)
+        return T["d%s_%d" % (item, j)][:]
+    load_w(0)
+    load_x(A, 0)
+    D.wait_ge(S.qw0, 1)
+    load_w(1)
+    D.wait_ge(S.qx0, 1)
+    load_x(D, 1)
+    D.dma_start(T.bv[:], T.w2[:]).then_inc(S.lv, 16)
+    for m in range(2, MB):
+        D.wait_ge(S["qx%d" % (m - 1)], 1)
+        load_x(D, m)
+    for q in range(MB // 2, NB // 2):
+        j, p = pairs[q]
+        if q >= PS:
+            D.wait_ge(S["m%d" % (2 * (q - PS) + 1)], 1)
+            if q - PS < MB // 2:
+                D.wait_ge(S["sp%d" % (q - PS)], left["p%d" % (q - PS)])
+        D.dma_start(T.hp[:, cols(q % PS, 2 * NC)], arrived("p%d" % p, j)).then_inc(S["f%d" % (2 * q)], 16)
+        for i in range(2):
+            k = 2 * q + i
+            D.wait_ge(S["m%d" % (k - HS)], 1)
+            if k - HS < MB:
+                D.wait_ge(S["sc%d" % (k - HS)], left["c%d" % (k - HS)])
+            src = arrived("c%d" % (2 * p + i), j)
+            D.dma_start(codes(k).bitcast(U8), src.bitcast(U8)).then_inc(S["f%d" % k], 16)
+
+    def product(m, i):
+        P.matmul_mx(bank(2 * (m % 2) + i), T.wc[:, cols(i)], T.wp[:, cols(i)], T.xc[:], T.xp[:],
+                    True, True).then_inc(S["z%d%d" % (i, m)], 1)
+
+    def block(k):
+        if k < MB:
+            P.wait_ge(S["qh%d" % k], 1)
+        else:
+            P.wait_ge(S["f%d" % k], 16 if k % 2 else 32)
+        if k >= 8:
+            P.wait_ge(S["k%d" % (k - 8)], 1)
+        P.matmul_mx(bank((4 + k) % 8), T.vc[:], T.vp[:], codes(k), plane(k), True, True).then_inc(S["m%d" % k], 1)
+
+    P.wait_ge(S.qw0, 1)
+    P.wait_ge(S.qx0, 1)
+    product(0, 0)
+    P.wait_ge(S.qw1, 1)
+    product(0, 1)
+    for m in range(1, MB):
+        P.wait_ge(S["qx%d" % m], 1)
+        if m >= 2:
+            P.wait_ge(S["qh%d" % (m - 2)], 1)
+        product(m, 0)
+        product(m, 1)
+        if m == 1:
+            P.wait_ge(S.qv, 1)
+            block(0)
+            block(1)
+    for k in range(2, NB):
+        block(k)
+
+    def quant_x(m):
+        V.wait_ge(S["lx%d" % m], 16)
+        if m:
+            V.wait_ge(S["z1%d" % (m - 1)], 1)
+        V.quantize_mx(T.xc[:], T.xp[:], T.bx[:]).then_inc(S["qx%d" % m], 1)
+
+    def quant_w(i):
+        V.wait_ge(S["lw%d" % i], 16)
+        V.quantize_mx(T.wc[:, cols(i)], T.wp[:, cols(i)], T.bw[:]).then_inc(S["qw%d" % i], 1)
+
+    def signs_v(m):
+        V.wait_ge(S["z0%d" % m], 1)
+        if m:
+            V.wait_ge(S["qh%d" % (m - 1)], 1)
+        for b, s in ((0, C), (1, -C)):
+            V.tensor_scalar(T.bh[:, b:512:4], bank(2 * (m % 2)), s, 0.0,
+                            AluOpType.mult, AluOpType.max).then_inc(S["sg%d" % m], 1)
+
+    def signs_s(m):
+        A.wait_ge(S["z1%d" % m], 1)
+        if m:
+            A.wait_ge(S["qh%d" % (m - 1)], 1)
+        for b, s in ((2, C), (3, -C)):
+            A.activation(T.bh[:, b:512:4], bank(2 * (m % 2) + 1), F.Relu, scale=s).then_inc(S["sg%d" % m], 1)
+
+    def quant_h(m):
+        V.wait_ge(S["sg%d" % m], 4)
+        if m >= HS:
+            V.wait_ge(S["m%d" % (m - HS)], 1)
+            V.wait_ge(S["sc%d" % (m - HS)], left["c%d" % (m - HS)])
+        V.quantize_mx(codes(m), plane(m), T.bh[:]).then_inc(S["qh%d" % m], 1)
+
+    def finish(q):
+        s = q % YS
+        for k, e in ((2 * q, V), (2 * q + 1, A)):
+            e.wait_ge(S["m%d" % k], 1)
+            if q >= YS:
+                e.wait_ge(S["y%d" % s], 16 * (q // YS))
+            out = T.ys[:, cols(2 * s + k % 2)]
+            if e is V:
+                V.tensor_copy(out, bank((4 + k) % 8)).then_inc(S["k%d" % k], 1)
+            else:
+                A.activation(out, bank((4 + k) % 8), F.Copy).then_inc(S["k%d" % k], 1)
+            A.wait_ge(S["k%d" % k], 1)
+        j, p = pairs[q]
+        at = NC * (MB * j + 2 * p)
+        A.dma_start(T.y[:, at:at + 2 * NC], T.ys[:, cols(s, 2 * NC)]).then_inc(S["y%d" % s], 16)
+
+    quant_w(0)
+    quant_x(0)
+    signs_v(0)
+    signs_s(0)
+    quant_w(1)
+    quant_x(1)
+    quant_h(0)
+    V.wait_ge(S.lv, 16)
+    V.quantize_mx(T.vc[:], T.vp[:], T.bv[:]).then_inc(S.qv, 1)
+    for m in range(1, MB):
+        if m > 1:
+            quant_x(m)
+        signs_v(m)
+        signs_s(m)
+        quant_h(m)
+        if m % 2:
+            finish(m // 2)
+    for q in range(MB // 2, NB // 2):
+        finish(q)
+    for s in range(YS):
+        A.wait_ge(S["y%d" % s], 16 * len(range(s, NB // 2, YS)))
+
+
+def helper_core(g, core, j, T, topo):
+    total = 0
+    way = roads(T, topo, j)
+    for item in ITEMS:
+        for carrier, es, ranks, eo in way[item]:
+            if carrier == core:
+                g.wait_ge(T.sem["s" + item], len(es))
+                total += send(g, T, topo, item, j, T["d%s_%d" % (item, j)][:],
+                              [(eo, [T.cores[r] for r in ranks], "a%s_%d" % (item, j))], T.sem.out)
+    if total:
+        g.wait_ge(T.sem.out, total)
+
+
+def rank_program(g, core, T, topo):
+    rank = T.rank_of(core)
+    if rank is not None:
+        rank_core(g, core, rank, T, topo)
+        return
+    for j in range(N):
+        if topo.chip(core) == topo.chip(T.cores[j]):
+            helper_core(g, core, j, T, topo)

@@ -2,12 +2,14 @@ from concourse.bass import DstId, RemoteDMATransfer
 from concourse.mybir import dt, AluOpType, ActivationFunctionType
 
 N, MB, NC = 6, 4, 128
-NB = N * MB
+NP, PC = 2, 2 * NC
+NQ = N * NP
 SIM_CORES = 112
 C = 0.029
 U8 = dt.uint8
-HS, PS, YS = 3, 3, 2
-ITEMS = ("c0", "p0", "c1", "c2", "p1", "c3")
+RING = (3, 2, 4, 1, 5)
+CODES = (("c0", "c1"), ("q1",))
+AFTER = (("c0",), ("p0", "c1"), (), ("p1", "q1"))
 
 SCRATCH = {
     "bw": ("sbuf", [128, 512], "bfloat16"),
@@ -15,66 +17,81 @@ SCRATCH = {
     "bx": ("sbuf", [128, 512], "bfloat16"),
     "bh": ("sbuf", [128, 512], "bfloat16"),
     "xc": ("sbuf", [128, NC], "float8_e4m3fn_x4"),
-    "xp": ("sbuf", [128, NC], "uint8"),
     "wc": ("sbuf", [128, 2 * NC], "float8_e4m3fn_x4"),
-    "wp": ("sbuf", [128, 2 * NC], "uint8"),
     "vc": ("sbuf", [128, NC], "float8_e4m3fn_x4"),
     "vp": ("sbuf", [128, NC], "uint8"),
-    "hc": ("sbuf", [128, HS * NC], "float8_e4m3fn_x4"),
-    "hp": ("sbuf", [128, PS * 2 * NC], "uint8"),
-    "ys": ("sbuf", [128, YS * 2 * NC], "float32"),
+    "hc": ("sbuf", [128, 2 * PC], "float8_e4m3fn_x4"),
+    "pl": ("sbuf", [128, 3 * PC], "uint8"),
+    "ys": ("sbuf", [128, 2 * PC], "float32"),
     "ps": ("psum", [128, 8 * 512], "float32"),
 }
-SEMAPHORES = ["lw0", "lw1", "lv", "qw0", "qw1", "qv", "out"]
+XP, WP = 3 * NC, 4 * NC
+SEMAPHORES = ["lw0", "lw1", "lv", "qw0", "qw1", "qv", "out", "y0", "y1"]
 SEMAPHORES += ["%s%d" % (_s, _m) for _s in ("lx", "qx", "z0", "z1", "sg", "qh") for _m in range(MB)]
-SEMAPHORES += ["%s%d" % (_s, _k) for _s in ("m", "k") for _k in range(NB)]
-SEMAPHORES += ["f%d" % _k for _k in range(MB, NB)]
-SEMAPHORES += ["y%d" % _s for _s in range(YS)]
-for _i in ITEMS:
+SEMAPHORES += ["%s%d" % (_s, _k) for _s in ("m", "k") for _k in range(2 * NQ)]
+SEMAPHORES += ["f%d" % _q for _q in range(NQ)]
+for _i in ("c0", "c1", "q1", "p0", "p1"):
     SEMAPHORES.append("s" + _i)
     for _j in range(N):
-        SEMAPHORES.append("a%s_%d" % (_i, _j))
-        SCRATCH["d%s_%d" % (_i, _j)] = (("dram", [128, NC], "float8_e4m3fn_x4") if _i[0] == "c"
-                                        else ("dram", [128, 2 * NC], "uint8"))
+        SEMAPHORES.append("a%s%d" % (_i, _j))
+        SCRATCH["d%s%d" % (_i, _j)] = ("dram", [128, NC if _i[0] == "c" else PC],
+                                       "uint8" if _i[0] == "p" else "float8_e4m3fn_x4")
 
 
 def engines(mask):
     return [i for i in range(mask.bit_length()) if (mask >> i) & 1]
 
 
+def byte_view(item, ap):
+    return ap if item[0] == "p" else ap.bitcast(U8)
+
+
 def roads(T, topo, j):
     home = T.cores[j]
     own = [c for c in range(SIM_CORES) if topo.chip(c) == topo.chip(home) and c not in T.cores
            and all(topo.may_write(c, q) for q in T.cores if q != c)]
-    near = [c for c in own if topo.die(c) == topo.die(home)]
-    far = [c for c in own if topo.die(c) != topo.die(home)]
-    rest = [(j + o) % N for o in range(1, N)]
-    same = [r for r in rest if topo.same_plane(topo.chip(T.cores[r]), topo.chip(home))]
-    cross = [r for r in rest if r not in same]
-    off = engines(topo.mask(home, T.cores[cross[0]]))
-    on = [e for e in engines(topo.mask(home, own[0])) if e not in off]
-    if len(same) > len(cross):
-        a, b = cross, same
-    else:
-        a, b = cross[0::2] + same, cross[1::2]
-    first = [(home, None, same, off), (far[0], on, cross, off)]
-    split = [(near[1], on[0::2], a, off), (far[1], on[1::2], b, off)]
-    return {"c0": first, "p0": first,
-            "c1": [(near[0], on, same + cross, off)],
-            "c2": [(far[0], on, same + cross, off)],
-            "p1": split, "c3": split}
+    near = [c for c in own if topo.die(c) == topo.die(home)][0]
+    far = [c for c in own if topo.die(c) != topo.die(home)][0]
+    ring = [(j + o) % N for o in RING]
+    same = [r for r in ring if topo.same_plane(topo.chip(T.cores[r]), topo.chip(home))]
+    same.sort(key=lambda r: (r - j) % N)
+    off = engines(topo.mask(home, T.cores[same[0]]))
+    wide = engines(topo.mask(home, near))
+    on = [e for e in wide if e not in off]
+    straight = (home, None, same[:1], off)
+    others = [r for r in ring if r != same[0]]
+    last = [(near, wide[0::2], ring[0::2], off), (far, wide[1::2], ring[1::2], off)]
+    return {"c0": [straight, (near, on, others, off)],
+            "p0": [straight, (far, on, others, off)],
+            "c1": [straight, (far, on, others, off)],
+            "p1": last, "q1": last}
+
+
+def arrivals(T, topo, item, j, rank):
+    return [len(eo) for c, es, ranks, eo in roads(T, topo, j)[item] if rank in ranks][0]
+
+
+def sequence(T, topo, rank):
+    js = [(rank - o) % N for o in RING]
+    first = sorted(js, key=lambda j: rank not in roads(T, topo, j)["c0"][0][2])
+    return [(rank, 0), (first[0], 0), (rank, 1)] + [(j, 0) for j in first[1:]] + [(j, 1) for j in js]
 
 
 def send(g, T, topo, item, j, src, parts, local):
-    land = T["d%s_%d" % (item, j)][:]
-    if item[0] == "c":
-        src, land = src.bitcast(U8), land.bitcast(U8)
+    dram = T["d%s%d" % (item, j)][:]
+
+    def land(c):
+        if item[0] == "c" and c in T.cores and sequence(T, topo, T.rank_of(c))[1][0] == j:
+            at = PC + NC * CODES[0].index(item)
+            return byte_view(item, T.hc[:, at:at + NC])
+        return byte_view(item, dram)
     trs = []
     for es, cores, sem in parts:
         ids = [topo.addr(c) for c in cores]
-        trs.append(RemoteDMATransfer(dst_ids=[DstId(rid=i[0], pnc=i[1]) for i in ids],
+        trs.append(RemoteDMATransfer(dst_ids=[DstId(rid=a[0], pnc=a[1]) for a in ids],
                                      dma_engine_mask=sum(1 << e for e in es), remote_sem=T.sem[sem],
-                                     srcs=[src], dsts=[land for c in cores]))
+                                     srcs=[byte_view(item, dram if src is None else src)],
+                                     dsts=[land(c) for c in cores]))
     g.remote_dma_fused(trs, local_sem=local)
     return sum(len(es) for es, cores, sem in parts)
 
@@ -83,89 +100,112 @@ def rank_core(g, core, rank, T, topo):
     S = T.sem
     V, P, A, D = g.vector, g.tensor, g.scalar, g.sync
     F = ActivationFunctionType
+    seq = sequence(T, topo, rank)
+    place = [seq.index((rank, p)) for p in range(NP)]
 
     def cols(s, n=NC):
         return slice(n * s, n * s + n)
 
-    def codes(k):
-        return T.hc[:, cols(k % HS)]
-
-    def plane(k):
-        return T.hp[:, cols(2 * (k // 2 % PS) + k % 2)]
-
     def bank(b):
         return T.ps[:, 512 * b:512 * b + NC]
 
+    def zbank(m, i):
+        return bank(2 * (m % 2) + i)
+
+    yb = [2, 3] + [(q + 2) % 4 for q in range(2, NQ)]
+    before = [max([i for i in range(q) if yb[i] == yb[q]], default=None) for q in range(NQ)]
+
+    def ybank(k):
+        return bank(2 * yb[k // 2] + k % 2)
+
+    def codes(q):
+        return T.hc[:, cols(q % 2, PC)]
+
+    def planes(q):
+        return T.pl[:, cols((0, 2, 1)[q % 3], PC)]
+
+    def tile_codes(k):
+        return T.hc[:, cols(k % 4)]
+
+    def tile_plane(k):
+        return T.pl[:, cols(2 * (0, 2, 1)[k // 2 % 3] + k % 2)]
+
     left = {}
-
-    def ship(item, src):
-        parts = []
-        for carrier, es, ranks, eo in roads(T, topo, rank)[item]:
-            if carrier == core:
-                parts.append((eo, [T.cores[r] for r in ranks], "a%s_%d" % (item, rank)))
-            else:
-                parts.append((es, [carrier], "s" + item))
-        left[item] = send(g, T, topo, item, rank, src, parts, S["s" + item])
     for m in range(MB):
-        g.wait_ge(S["qh%d" % m], 1)
-        if m % 2:
-            ship("p%d" % (m // 2), T.hp[:, cols(m // 2, 2 * NC)])
-        ship("c%d" % m, codes(m))
+        if AFTER[m]:
+            g.wait_ge(S["qh%d" % m], 1)
+        for item in AFTER[m]:
+            parts = []
+            for carrier, es, ranks, eo in roads(T, topo, rank)[item]:
+                if carrier == core:
+                    parts.append((eo, [T.cores[r] for r in ranks], "a%s%d" % (item, rank)))
+                else:
+                    parts.append((es, [carrier], "s" + item))
+            q = place[m // 2]
+            src = planes(q) if item[0] == "p" else codes(q) if item[0] == "q" else tile_codes(2 * q + m % 2)
+            left[item] = send(g, T, topo, item, rank, src, parts, S["s" + item])
 
-    pairs = [(rank, p) for p in range(MB // 2)]
-    for p in range(MB // 2):
-        js = [(rank - o) % N for o in range(1, N)]
-        if p == 0:
-            js.sort(key=lambda j: not topo.same_plane(topo.chip(T.cores[j]), topo.chip(core)))
-        pairs += [(j, p) for j in js]
+    def gone(e, items):
+        for item in items:
+            e.wait_ge(S["s" + item], left[item])
 
-    def load_x(q, m):
-        q.dma_start(T.bx[:], T.x[:, cols(m, 512)]).then_inc(S["lx%d" % m], 16)
+    def load_x(m):
+        D.dma_start(T.bx[:], T.x[:, cols(m, 512)]).then_inc(S["lx%d" % m], 16)
 
     def load_w(i):
         D.dma_start(T.bw[:], T.w1[:, cols(i, 512)]).then_inc(S["lw%d" % i], 16)
 
-    def arrived(item, j):
-        n = [len(eo) for c, es, ranks, eo in roads(T, topo, j)[item] if rank in ranks][0]
-        D.wait_ge(S["a%s_%d" % (item, j)], n)
-        return T["d%s_%d" % (item, j)][:]
+    def fetch(q, item, out):
+        j = seq[q][0]
+        D.wait_ge(S["a%s%d" % (item, j)], arrivals(T, topo, item, j, rank))
+        D.dma_start(byte_view(item, out), byte_view(item, T["d%s%d" % (item, j)][:])).then_inc(S["f%d" % q], 16)
+
     load_w(0)
-    load_x(A, 0)
+    load_x(0)
     D.wait_ge(S.qw0, 1)
     load_w(1)
-    D.wait_ge(S.qx0, 1)
-    load_x(D, 1)
-    D.dma_start(T.bv[:], T.w2[:]).then_inc(S.lv, 16)
-    for m in range(2, MB):
+    for m in range(1, MB):
         D.wait_ge(S["qx%d" % (m - 1)], 1)
-        load_x(D, m)
-    for q in range(MB // 2, NB // 2):
-        j, p = pairs[q]
-        if q >= PS:
-            D.wait_ge(S["m%d" % (2 * (q - PS) + 1)], 1)
-            if q - PS < MB // 2:
-                D.wait_ge(S["sp%d" % (q - PS)], left["p%d" % (q - PS)])
-        D.dma_start(T.hp[:, cols(q % PS, 2 * NC)], arrived("p%d" % p, j)).then_inc(S["f%d" % (2 * q)], 16)
-        for i in range(2):
-            k = 2 * q + i
-            D.wait_ge(S["m%d" % (k - HS)], 1)
-            if k - HS < MB:
-                D.wait_ge(S["sc%d" % (k - HS)], left["c%d" % (k - HS)])
-            src = arrived("c%d" % (2 * p + i), j)
-            D.dma_start(codes(k).bitcast(U8), src.bitcast(U8)).then_inc(S["f%d" % k], 16)
+        load_x(m)
+        if m == 1:
+            D.dma_start(T.bv[:], T.w2[:]).then_inc(S.lv, 16)
+    D.wait_ge(S["z1%d" % (MB - 1)], 1)
+    fetched = [0] * NQ
+    for q in range(NQ):
+        if q in place:
+            continue
+        p = seq[q][1]
+        if q >= 3:
+            D.wait_ge(S["m%d" % (2 * (q - 3) + 1)], 1)
+            if q - 3 in place:
+                gone(D, ["p%d" % place.index(q - 3)])
+        fetch(q, "p%d" % p, planes(q))
+        fetched[q] = 16
+        if q == 1:
+            continue
+        D.wait_ge(S["m%d" % (2 * (q - 2) + 1)], 1)
+        if q - 2 in place:
+            gone(D, CODES[place.index(q - 2)])
+        for n, item in enumerate(CODES[p]):
+            fetch(q, item, codes(q) if len(CODES[p]) == 1 else tile_codes(2 * q + n))
+            fetched[q] += 16
 
     def product(m, i):
-        P.matmul_mx(bank(2 * (m % 2) + i), T.wc[:, cols(i)], T.wp[:, cols(i)], T.xc[:], T.xp[:],
-                    True, True).then_inc(S["z%d%d" % (i, m)], 1)
+        P.matmul_mx(zbank(m, i), T.wc[:, cols(i)], T.pl[:, WP + NC * i:WP + NC * i + NC], T.xc[:],
+                    T.pl[:, XP:XP + NC], True, True).then_inc(S["z%d%d" % (i, m)], 1)
 
-    def block(k):
-        if k < MB:
-            P.wait_ge(S["qh%d" % k], 1)
-        else:
-            P.wait_ge(S["f%d" % k], 16 if k % 2 else 32)
-        if k >= 8:
-            P.wait_ge(S["k%d" % (k - 8)], 1)
-        P.matmul_mx(bank((4 + k) % 8), T.vc[:], T.vp[:], codes(k), plane(k), True, True).then_inc(S["m%d" % k], 1)
+    def block(q):
+        if q not in place:
+            P.wait_ge(S["f%d" % q], fetched[q])
+        if q == 1:
+            for item in CODES[0]:
+                P.wait_ge(S["a%s%d" % (item, seq[1][0])], arrivals(T, topo, item, seq[1][0], rank))
+        for k in (2 * q, 2 * q + 1):
+            if q in place:
+                P.wait_ge(S["qh%d" % (2 * place.index(q) + k % 2)], 1)
+            if before[q] is not None:
+                P.wait_ge(S["k%d" % (2 * before[q] + k % 2)], 1)
+            P.matmul_mx(ybank(k), T.vc[:], T.vp[:], tile_codes(k), tile_plane(k), True, True).then_inc(S["m%d" % k], 1)
 
     P.wait_ge(S.qw0, 1)
     P.wait_ge(S.qx0, 1)
@@ -181,26 +221,25 @@ def rank_core(g, core, rank, T, topo):
         if m == 1:
             P.wait_ge(S.qv, 1)
             block(0)
-            block(1)
-    for k in range(2, NB):
-        block(k)
+    for q in range(1, NQ):
+        block(q)
 
     def quant_x(m):
         V.wait_ge(S["lx%d" % m], 16)
         if m:
             V.wait_ge(S["z1%d" % (m - 1)], 1)
-        V.quantize_mx(T.xc[:], T.xp[:], T.bx[:]).then_inc(S["qx%d" % m], 1)
+        V.quantize_mx(T.xc[:], T.pl[:, XP:XP + NC], T.bx[:]).then_inc(S["qx%d" % m], 1)
 
     def quant_w(i):
         V.wait_ge(S["lw%d" % i], 16)
-        V.quantize_mx(T.wc[:, cols(i)], T.wp[:, cols(i)], T.bw[:]).then_inc(S["qw%d" % i], 1)
+        V.quantize_mx(T.wc[:, cols(i)], T.pl[:, WP + NC * i:WP + NC * i + NC], T.bw[:]).then_inc(S["qw%d" % i], 1)
 
     def signs_v(m):
         V.wait_ge(S["z0%d" % m], 1)
         if m:
             V.wait_ge(S["qh%d" % (m - 1)], 1)
         for b, s in ((0, C), (1, -C)):
-            V.tensor_scalar(T.bh[:, b:512:4], bank(2 * (m % 2)), s, 0.0,
+            V.tensor_scalar(T.bh[:, b:512:4], zbank(m, 0), s, 0.0,
                             AluOpType.mult, AluOpType.max).then_inc(S["sg%d" % m], 1)
 
     def signs_s(m):
@@ -208,30 +247,34 @@ def rank_core(g, core, rank, T, topo):
         if m:
             A.wait_ge(S["qh%d" % (m - 1)], 1)
         for b, s in ((2, C), (3, -C)):
-            A.activation(T.bh[:, b:512:4], bank(2 * (m % 2) + 1), F.Relu, scale=s).then_inc(S["sg%d" % m], 1)
+            A.activation(T.bh[:, b:512:4], zbank(m, 1), F.Relu, scale=s).then_inc(S["sg%d" % m], 1)
 
     def quant_h(m):
         V.wait_ge(S["sg%d" % m], 4)
-        if m >= HS:
-            V.wait_ge(S["m%d" % (m - HS)], 1)
-            V.wait_ge(S["sc%d" % (m - HS)], left["c%d" % (m - HS)])
-        V.quantize_mx(codes(m), plane(m), T.bh[:]).then_inc(S["qh%d" % m], 1)
+        if m == 2:
+            V.wait_ge(S.m1, 1)
+            gone(V, CODES[0])
+        if m == 3:
+            V.wait_ge(S["z1%d" % m], 1)
+        k = 2 * place[m // 2] + m % 2
+        V.quantize_mx(tile_codes(k), tile_plane(k), T.bh[:]).then_inc(S["qh%d" % m], 1)
 
     def finish(q):
-        s = q % YS
+        s = q % 2
         for k, e in ((2 * q, V), (2 * q + 1, A)):
             e.wait_ge(S["m%d" % k], 1)
-            if q >= YS:
-                e.wait_ge(S["y%d" % s], 16 * (q // YS))
+            if q >= 2:
+                e.wait_ge(S["y%d" % s], 16 * (q // 2))
             out = T.ys[:, cols(2 * s + k % 2)]
             if e is V:
-                V.tensor_copy(out, bank((4 + k) % 8)).then_inc(S["k%d" % k], 1)
+                V.tensor_copy(out, ybank(k)).then_inc(S["k%d" % k], 1)
             else:
-                A.activation(out, bank((4 + k) % 8), F.Copy).then_inc(S["k%d" % k], 1)
+                A.activation(out, ybank(k), F.Copy).then_inc(S["k%d" % k], 1)
+        for k in (2 * q, 2 * q + 1):
             A.wait_ge(S["k%d" % k], 1)
-        j, p = pairs[q]
+        j, p = seq[q]
         at = NC * (MB * j + 2 * p)
-        A.dma_start(T.y[:, at:at + 2 * NC], T.ys[:, cols(s, 2 * NC)]).then_inc(S["y%d" % s], 16)
+        A.dma_start(T.y[:, at:at + PC], T.ys[:, cols(s, PC)]).then_inc(S["y%d" % s], 16)
 
     quant_w(0)
     quant_x(0)
@@ -240,31 +283,35 @@ def rank_core(g, core, rank, T, topo):
     quant_w(1)
     quant_x(1)
     quant_h(0)
+    signs_v(1)
+    signs_s(1)
+    quant_h(1)
     V.wait_ge(S.lv, 16)
     V.quantize_mx(T.vc[:], T.vp[:], T.bv[:]).then_inc(S.qv, 1)
-    for m in range(1, MB):
-        if m > 1:
-            quant_x(m)
-        signs_v(m)
-        signs_s(m)
-        quant_h(m)
-        if m % 2:
-            finish(m // 2)
-    for q in range(MB // 2, NB // 2):
+    quant_x(2)
+    signs_v(2)
+    signs_s(2)
+    finish(0)
+    quant_x(3)
+    quant_h(2)
+    signs_v(3)
+    signs_s(3)
+    quant_h(3)
+    for q in range(1, NQ):
         finish(q)
-    for s in range(YS):
-        A.wait_ge(S["y%d" % s], 16 * len(range(s, NB // 2, YS)))
+    for s in range(2):
+        A.wait_ge(S["y%d" % s], 16 * (NQ // 2))
 
 
 def helper_core(g, core, j, T, topo):
     total = 0
     way = roads(T, topo, j)
-    for item in ITEMS:
+    for item in [i for items in AFTER for i in items]:
         for carrier, es, ranks, eo in way[item]:
             if carrier == core:
                 g.wait_ge(T.sem["s" + item], len(es))
-                total += send(g, T, topo, item, j, T["d%s_%d" % (item, j)][:],
-                              [(eo, [T.cores[r] for r in ranks], "a%s_%d" % (item, j))], T.sem.out)
+                total += send(g, T, topo, item, j, None,
+                              [(eo, [T.cores[r] for r in ranks], "a%s%d" % (item, j))], T.sem.out)
     if total:
         g.wait_ge(T.sem.out, total)
 

from concourse.bass import DstId, RemoteDMATransfer
from concourse.mybir import dt, AluOpType, ActivationFunctionType

N, MB, NC = 6, 4, 128
NP, PC = 2, 2 * NC
NQ = N * NP
SIM_CORES = 112
C = 0.029
U8 = dt.uint8
RING = (3, 2, 4, 1, 5)
CODES = (("c0", "c1"), ("q1",))
AFTER = (("c0",), ("p0", "c1"), (), ("p1", "q1"))

SCRATCH = {
    "bw": ("sbuf", [128, 512], "bfloat16"),
    "bv": ("sbuf", [128, 512], "bfloat16"),
    "bx": ("sbuf", [128, 512], "bfloat16"),
    "bh": ("sbuf", [128, 512], "bfloat16"),
    "xc": ("sbuf", [128, NC], "float8_e4m3fn_x4"),
    "wc": ("sbuf", [128, 2 * NC], "float8_e4m3fn_x4"),
    "vc": ("sbuf", [128, NC], "float8_e4m3fn_x4"),
    "vp": ("sbuf", [128, NC], "uint8"),
    "hc": ("sbuf", [128, 2 * PC], "float8_e4m3fn_x4"),
    "pl": ("sbuf", [128, 3 * PC], "uint8"),
    "ys": ("sbuf", [128, 2 * PC], "float32"),
    "ps": ("psum", [128, 8 * 512], "float32"),
}
XP, WP = 3 * NC, 4 * NC
SEMAPHORES = ["lw0", "lw1", "lv", "qw0", "qw1", "qv", "out", "y0", "y1"]
SEMAPHORES += ["%s%d" % (_s, _m) for _s in ("lx", "qx", "z0", "z1", "sg", "qh") for _m in range(MB)]
SEMAPHORES += ["%s%d" % (_s, _k) for _s in ("m", "k") for _k in range(2 * NQ)]
SEMAPHORES += ["f%d" % _q for _q in range(NQ)]
for _i in ("c0", "c1", "q1", "p0", "p1"):
    SEMAPHORES.append("s" + _i)
    for _j in range(N):
        SEMAPHORES.append("a%s%d" % (_i, _j))
        SCRATCH["d%s%d" % (_i, _j)] = ("dram", [128, NC if _i[0] == "c" else PC],
                                       "uint8" if _i[0] == "p" else "float8_e4m3fn_x4")


def engines(mask):
    return [i for i in range(mask.bit_length()) if (mask >> i) & 1]


def byte_view(item, ap):
    return ap if item[0] == "p" else ap.bitcast(U8)


def roads(T, topo, j):
    home = T.cores[j]
    own = [c for c in range(SIM_CORES) if topo.chip(c) == topo.chip(home) and c not in T.cores
           and all(topo.may_write(c, q) for q in T.cores if q != c)]
    near = [c for c in own if topo.die(c) == topo.die(home)][0]
    far = [c for c in own if topo.die(c) != topo.die(home)][0]
    ring = [(j + o) % N for o in RING]
    same = [r for r in ring if topo.same_plane(topo.chip(T.cores[r]), topo.chip(home))]
    same.sort(key=lambda r: (r - j) % N)
    off = engines(topo.mask(home, T.cores[same[0]]))
    wide = engines(topo.mask(home, near))
    on = [e for e in wide if e not in off]
    straight = (home, None, same[:1], off)
    others = [r for r in ring if r != same[0]]
    last = [(near, wide[0::2], ring[0::2], off), (far, wide[1::2], ring[1::2], off)]
    return {"c0": [straight, (near, on, others, off)],
            "p0": [straight, (far, on, others, off)],
            "c1": [straight, (far, on, others, off)],
            "p1": last, "q1": last}


def arrivals(T, topo, item, j, rank):
    return [len(eo) for c, es, ranks, eo in roads(T, topo, j)[item] if rank in ranks][0]


def sequence(T, topo, rank):
    js = [(rank - o) % N for o in RING]
    first = sorted(js, key=lambda j: rank not in roads(T, topo, j)["c0"][0][2])
    return [(rank, 0), (first[0], 0), (rank, 1)] + [(j, 0) for j in first[1:]] + [(j, 1) for j in js]


def send(g, T, topo, item, j, src, parts, local):
    dram = T["d%s%d" % (item, j)][:]

    def land(c):
        if item[0] == "c" and c in T.cores and sequence(T, topo, T.rank_of(c))[1][0] == j:
            at = PC + NC * CODES[0].index(item)
            return byte_view(item, T.hc[:, at:at + NC])
        return byte_view(item, dram)
    trs = []
    for es, cores, sem in parts:
        ids = [topo.addr(c) for c in cores]
        trs.append(RemoteDMATransfer(dst_ids=[DstId(rid=a[0], pnc=a[1]) for a in ids],
                                     dma_engine_mask=sum(1 << e for e in es), remote_sem=T.sem[sem],
                                     srcs=[byte_view(item, dram if src is None else src)],
                                     dsts=[land(c) for c in cores]))
    g.remote_dma_fused(trs, local_sem=local)
    return sum(len(es) for es, cores, sem in parts)


def rank_core(g, core, rank, T, topo):
    S = T.sem
    V, P, A, D = g.vector, g.tensor, g.scalar, g.sync
    F = ActivationFunctionType
    seq = sequence(T, topo, rank)
    place = [seq.index((rank, p)) for p in range(NP)]

    def cols(s, n=NC):
        return slice(n * s, n * s + n)

    def bank(b):
        return T.ps[:, 512 * b:512 * b + NC]

    def zbank(m, i):
        return bank(2 * (m % 2) + i)

    yb = [2, 3] + [(q + 2) % 4 for q in range(2, NQ)]
    before = [max([i for i in range(q) if yb[i] == yb[q]], default=None) for q in range(NQ)]

    def ybank(k):
        return bank(2 * yb[k // 2] + k % 2)

    def codes(q):
        return T.hc[:, cols(q % 2, PC)]

    def planes(q):
        return T.pl[:, cols((0, 2, 1)[q % 3], PC)]

    def tile_codes(k):
        return T.hc[:, cols(k % 4)]

    def tile_plane(k):
        return T.pl[:, cols(2 * (0, 2, 1)[k // 2 % 3] + k % 2)]

    left = {}
    for m in range(MB):
        if AFTER[m]:
            g.wait_ge(S["qh%d" % m], 1)
        for item in AFTER[m]:
            parts = []
            for carrier, es, ranks, eo in roads(T, topo, rank)[item]:
                if carrier == core:
                    parts.append((eo, [T.cores[r] for r in ranks], "a%s%d" % (item, rank)))
                else:
                    parts.append((es, [carrier], "s" + item))
            q = place[m // 2]
            src = planes(q) if item[0] == "p" else codes(q) if item[0] == "q" else tile_codes(2 * q + m % 2)
            left[item] = send(g, T, topo, item, rank, src, parts, S["s" + item])

    def gone(e, items):
        for item in items:
            e.wait_ge(S["s" + item], left[item])

    def load_x(m):
        D.dma_start(T.bx[:], T.x[:, cols(m, 512)]).then_inc(S["lx%d" % m], 16)

    def load_w(i):
        D.dma_start(T.bw[:], T.w1[:, cols(i, 512)]).then_inc(S["lw%d" % i], 16)

    def fetch(q, item, out):
        j = seq[q][0]
        D.wait_ge(S["a%s%d" % (item, j)], arrivals(T, topo, item, j, rank))
        D.dma_start(byte_view(item, out), byte_view(item, T["d%s%d" % (item, j)][:])).then_inc(S["f%d" % q], 16)

    load_w(0)
    load_x(0)
    D.wait_ge(S.qw0, 1)
    load_w(1)
    for m in range(1, MB):
        D.wait_ge(S["qx%d" % (m - 1)], 1)
        load_x(m)
        if m == 1:
            D.dma_start(T.bv[:], T.w2[:]).then_inc(S.lv, 16)
    D.wait_ge(S["z1%d" % (MB - 1)], 1)
    fetched = [0] * NQ
    for q in range(NQ):
        if q in place:
            continue
        p = seq[q][1]
        if q >= 3:
            D.wait_ge(S["m%d" % (2 * (q - 3) + 1)], 1)
            if q - 3 in place:
                gone(D, ["p%d" % place.index(q - 3)])
        fetch(q, "p%d" % p, planes(q))
        fetched[q] = 16
        if q == 1:
            continue
        D.wait_ge(S["m%d" % (2 * (q - 2) + 1)], 1)
        if q - 2 in place:
            gone(D, CODES[place.index(q - 2)])
        for n, item in enumerate(CODES[p]):
            fetch(q, item, codes(q) if len(CODES[p]) == 1 else tile_codes(2 * q + n))
            fetched[q] += 16

    def product(m, i):
        P.matmul_mx(zbank(m, i), T.wc[:, cols(i)], T.pl[:, WP + NC * i:WP + NC * i + NC], T.xc[:],
                    T.pl[:, XP:XP + NC], True, True).then_inc(S["z%d%d" % (i, m)], 1)

    def block(q):
        if q not in place:
            P.wait_ge(S["f%d" % q], fetched[q])
        if q == 1:
            for item in CODES[0]:
                P.wait_ge(S["a%s%d" % (item, seq[1][0])], arrivals(T, topo, item, seq[1][0], rank))
        for k in (2 * q, 2 * q + 1):
            if q in place:
                P.wait_ge(S["qh%d" % (2 * place.index(q) + k % 2)], 1)
            if before[q] is not None:
                P.wait_ge(S["k%d" % (2 * before[q] + k % 2)], 1)
            P.matmul_mx(ybank(k), T.vc[:], T.vp[:], tile_codes(k), tile_plane(k), True, True).then_inc(S["m%d" % k], 1)

    P.wait_ge(S.qw0, 1)
    P.wait_ge(S.qx0, 1)
    product(0, 0)
    P.wait_ge(S.qw1, 1)
    product(0, 1)
    for m in range(1, MB):
        P.wait_ge(S["qx%d" % m], 1)
        if m >= 2:
            P.wait_ge(S["qh%d" % (m - 2)], 1)
        product(m, 0)
        product(m, 1)
        if m == 1:
            P.wait_ge(S.qv, 1)
            block(0)
    for q in range(1, NQ):
        block(q)

    def quant_x(m):
        V.wait_ge(S["lx%d" % m], 16)
        if m:
            V.wait_ge(S["z1%d" % (m - 1)], 1)
        V.quantize_mx(T.xc[:], T.pl[:, XP:XP + NC], T.bx[:]).then_inc(S["qx%d" % m], 1)

    def quant_w(i):
        V.wait_ge(S["lw%d" % i], 16)
        V.quantize_mx(T.wc[:, cols(i)], T.pl[:, WP + NC * i:WP + NC * i + NC], T.bw[:]).then_inc(S["qw%d" % i], 1)

    def signs_v(m):
        V.wait_ge(S["z0%d" % m], 1)
        if m:
            V.wait_ge(S["qh%d" % (m - 1)], 1)
        for b, s in ((0, C), (1, -C)):
            V.tensor_scalar(T.bh[:, b:512:4], zbank(m, 0), s, 0.0,
                            AluOpType.mult, AluOpType.max).then_inc(S["sg%d" % m], 1)

    def signs_s(m):
        A.wait_ge(S["z1%d" % m], 1)
        if m:
            A.wait_ge(S["qh%d" % (m - 1)], 1)
        for b, s in ((2, C), (3, -C)):
            A.activation(T.bh[:, b:512:4], zbank(m, 1), F.Relu, scale=s).then_inc(S["sg%d" % m], 1)

    def quant_h(m):
        V.wait_ge(S["sg%d" % m], 4)
        if m == 2:
            V.wait_ge(S.m1, 1)
            gone(V, CODES[0])
        if m == 3:
            V.wait_ge(S["z1%d" % m], 1)
        k = 2 * place[m // 2] + m % 2
        V.quantize_mx(tile_codes(k), tile_plane(k), T.bh[:]).then_inc(S["qh%d" % m], 1)

    def finish(q):
        s = q % 2
        for k, e in ((2 * q, V), (2 * q + 1, A)):
            e.wait_ge(S["m%d" % k], 1)
            if q >= 2:
                e.wait_ge(S["y%d" % s], 16 * (q // 2))
            out = T.ys[:, cols(2 * s + k % 2)]
            if e is V:
                V.tensor_copy(out, ybank(k)).then_inc(S["k%d" % k], 1)
            else:
                A.activation(out, ybank(k), F.Copy).then_inc(S["k%d" % k], 1)
        for k in (2 * q, 2 * q + 1):
            A.wait_ge(S["k%d" % k], 1)
        j, p = seq[q]
        at = NC * (MB * j + 2 * p)
        A.dma_start(T.y[:, at:at + PC], T.ys[:, cols(s, PC)]).then_inc(S["y%d" % s], 16)

    quant_w(0)
    quant_x(0)
    signs_v(0)
    signs_s(0)
    quant_w(1)
    quant_x(1)
    quant_h(0)
    signs_v(1)
    signs_s(1)
    quant_h(1)
    V.wait_ge(S.lv, 16)
    V.quantize_mx(T.vc[:], T.vp[:], T.bv[:]).then_inc(S.qv, 1)
    quant_x(2)
    signs_v(2)
    signs_s(2)
    finish(0)
    quant_x(3)
    quant_h(2)
    signs_v(3)
    signs_s(3)
    quant_h(3)
    for q in range(1, NQ):
        finish(q)
    for s in range(2):
        A.wait_ge(S["y%d" % s], 16 * (NQ // 2))


def helper_core(g, core, j, T, topo):
    total = 0
    way = roads(T, topo, j)
    for item in [i for items in AFTER for i in items]:
        for carrier, es, ranks, eo in way[item]:
            if carrier == core:
                g.wait_ge(T.sem["s" + item], len(es))
                total += send(g, T, topo, item, j, None,
                              [(eo, [T.cores[r] for r in ranks], "a%s%d" % (item, j))], T.sem.out)
    if total:
        g.wait_ge(T.sem.out, total)


def rank_program(g, core, T, topo):
    rank = T.rank_of(core)
    if rank is not None:
        rank_core(g, core, rank, T, topo)
        return
    for j in range(N):
        if topo.chip(core) == topo.chip(T.cores[j]):
            helper_core(g, core, j, T, topo)
